import numpy as np
CORES = [0,1,16,17,32,33,48,49,64,65,80,81,96,97,112,113,136,137,152,153,168,169,184,185,200,201,216,217,232,233,248,249]
N = 32
def setup_inputs(rng):
    return {"x": rng.standard_normal((N, 128, 1024)).astype(np.float32)}
def reference(x):
    b = 1024 // N
    blocks = x.reshape(N, 128, N, b)
    return {"y": np.ascontiguousarray(blocks.transpose(2, 1, 0, 3)).reshape(N, 128, 1024)}

@@ -1,0 +1,115 @@
+from concourse.bass import DstId, RemoteDMATransfer
+
+NB = 32
+B = 32
+
+SCRATCH = {
+    "src": ("sbuf", [128, NB * B], "float32"),
+    "land": ("sbuf", [128, NB * B], "float32"),
+}
+SEMAPHORES = ["loaded", "own", "sent", "arrived", "stored"]
+
+MATE_PORT = (2, 3, 6, 7)
+
+
+def world(host, chip, core):
+    return host * 128 + chip * 8 + core
+
+
+def rank_core(r):
+    h, k, c = r // 16, (r % 16) // 2, r % 2
+    return world(h, 2 * k + h, c)
+
+
+def plan():
+    writes = {}
+    used = {}
+
+    def put(core, dst, src_col, dst_col, n):
+        writes.setdefault(core, []).append((dst, src_col, dst_col, n))
+
+    def via(r, helper, first, n):
+        slot = used.get(helper, 0)
+        used[helper] = slot + n * B
+        put(rank_core(r), helper, first * B, slot, n)
+        for i in range(n):
+            put(helper, rank_core(first + i), slot + i * B, r * B, 1)
+
+    for r in range(NB):
+        h, k, c = r // 16, (r % 16) // 2, r % 2
+        chip = 2 * k + h
+        mine, other = 16 * h, 16 * (1 - h)
+        die_a, die_b, die_b_port = world(h, chip, 2 + c), world(h, chip, 4 + c), world(h, chip, 6 + c)
+        put(rank_core(r), rank_core(r ^ 1), (r ^ 1) * B, r * B, 1)
+        via(r, die_a if c == 0 else die_b_port, mine + 2 * (k ^ 1), 2)
+        pair = k // 2
+        via(r, die_a, mine + 4 * ((pair + 1) % 4), 4)
+        via(r, die_b, mine + 4 * ((pair + 2) % 4), 4)
+        via(r, die_b, mine + 4 * ((pair + 3) % 4), 4)
+        half = k // 4
+        base = other + 8 * half
+        via(r, die_a, base + 4 * c, 4)
+        via(r, die_b_port, base + 4 * (1 - c), 4)
+        for m in range(4 * (1 - half), 4 * (1 - half) + 4):
+            via(r, world(1 - h, 2 * m + h, MATE_PORT[k % 4]), other + 2 * m, 2)
+    return writes
+
+
+def calls_of(core, writes):
+    calls = []
+    for n in sorted({w[3] for w in writes}):
+        off = [w for w in writes if w[3] == n and w[0] // 8 != core // 8]
+        on = [w for w in writes if w[3] == n and w[0] // 8 == core // 8]
+        while off or on:
+            take_off, off = off[:8], off[8:]
+            e_off = 8
+            while take_off and e_off * len(take_off) > 8:
+                e_off //= 2
+            first_on = e_off * len(take_off)
+            take_on, on = on[:16 - first_on], on[16 - first_on:]
+            e_on = 16
+            while take_on and e_on * len(take_on) > 16 - first_on:
+                e_on //= 2
+            call, bit = [], 0
+            for group, e in ((take_off, e_off), (take_on, e_on)):
+                for w in group:
+                    call.append(w + (((1 << e) - 1) << bit, e))
+                    bit += e
+            calls.append(call)
+    return calls
+
+
+def rank_program(g, core, T, topo):
+    writes = plan()
+    all_calls = {c: calls_of(c, w) for c, w in writes.items()}
+    if core not in all_calls:
+        return
+    arriving = sum(t[5] for calls in all_calls.values() for call in calls for t in call if t[0] == core)
+    rank = T.rank_of(core)
+
+    if rank is not None:
+        g.dma_start(T.src[:], T.x[:]).then_inc(T.sem.loaded, 16)
+        g.dma_start(T.land[:, rank * B:(rank + 1) * B], T.x[:, rank * B:(rank + 1) * B]).then_inc(T.sem.own, 16)
+        g.wait_ge(T.sem.loaded, 16)
+        source = T.src
+    else:
+        g.wait_ge(T.sem.arrived, arriving)
+        source = T.land
+
+    leaving = 0
+    for call in all_calls[core]:
+        transfers = []
+        for dst, src_col, dst_col, n, mask, engines in call:
+            rid, pid = topo.addr(dst, core)
+            transfers.append(RemoteDMATransfer(
+                dst_ids=[DstId(rid=rid, pnc=pid)], dma_engine_mask=mask, remote_sem=T.sem.arrived,
+                src=source[:, src_col:src_col + n * B], dst=T.land[:, dst_col:dst_col + n * B]))
+            leaving += engines
+        g.remote_dma_fused(transfers, local_sem=T.sem.sent)
+
+    if rank is not None:
+        g.wait_ge(T.sem.arrived, arriving)
+        g.wait_ge(T.sem.own, 16)
+        g.dma_start(T.y[:], T.land[:]).then_inc(T.sem.stored, 16)
+        g.wait_ge(T.sem.stored, 16)
+    g.wait_ge(T.sem.sent, leaving)

@@ -7,7 +7,7 @@ SCRATCH = {
     "src": ("sbuf", [128, NB * B], "float32"),
     "land": ("sbuf", [128, NB * B], "float32"),
 }
-SEMAPHORES = ["loaded", "own", "sent", "arrived", "stored"]
+SEMAPHORES = ["ld_far", "ld_near", "own", "sent", "arr_a", "arr_b", "arr_s", "stored"]
 
 MATE_PORT = (2, 3, 6, 7)
 
@@ -22,94 +22,116 @@ def rank_core(r):
 
 
 def plan():
-    writes = {}
+    phases = {}
     used = {}
 
-    def put(core, dst, src_col, dst_col, n):
-        writes.setdefault(core, []).append((dst, src_col, dst_col, n))
+    def put(core, cls, dst, src_col, dst_col, n):
+        phases.setdefault(core, {}).setdefault(cls, []).append((dst, src_col, dst_col, n))
 
-    def via(r, helper, first, n):
+    def via(r, cls, helper, first, n):
         slot = used.get(helper, 0)
         used[helper] = slot + n * B
-        put(rank_core(r), helper, first * B, slot, n)
+        put(rank_core(r), cls, helper, first * B, slot, n)
         for i in range(n):
-            put(helper, rank_core(first + i), slot + i * B, r * B, 1)
+            if first + i != r:
+                put(helper, cls, rank_core(first + i), slot + i * B, r * B, 1)
 
     for r in range(NB):
         h, k, c = r // 16, (r % 16) // 2, r % 2
         chip = 2 * k + h
         mine, other = 16 * h, 16 * (1 - h)
         die_a, die_b, die_b_port = world(h, chip, 2 + c), world(h, chip, 4 + c), world(h, chip, 6 + c)
-        put(rank_core(r), rank_core(r ^ 1), (r ^ 1) * B, r * B, 1)
-        via(r, die_a if c == 0 else die_b_port, mine + 2 * (k ^ 1), 2)
-        pair = k // 2
-        via(r, die_a, mine + 4 * ((pair + 1) % 4), 4)
-        via(r, die_b, mine + 4 * ((pair + 2) % 4), 4)
-        via(r, die_b, mine + 4 * ((pair + 3) % 4), 4)
-        half = k // 4
-        base = other + 8 * half
-        via(r, die_a, base + 4 * c, 4)
-        via(r, die_b_port, base + 4 * (1 - c), 4)
+        pair, half = k // 2, k // 4
         for m in range(4 * (1 - half), 4 * (1 - half) + 4):
-            via(r, world(1 - h, 2 * m + h, MATE_PORT[k % 4]), other + 2 * m, 2)
-    return writes
+            via(r, "b", world(1 - h, 2 * m + h, MATE_PORT[k % 4]), other + 2 * m, 2)
+        base = other + 8 * half
+        via(r, "a", die_a, base + 4 * c, 4)
+        via(r, "a", die_b_port, base + 4 * (1 - c), 4)
+        via(r, "s", die_a if c == 0 else die_b_port, mine + 4 * pair, 4)
+        via(r, "s", die_a, mine + 4 * ((pair + 1) % 4), 4)
+        via(r, "s", die_b, mine + 4 * ((pair + 2) % 4), 4)
+        via(r, "s", die_b, mine + 4 * ((pair + 3) % 4), 4)
+    return phases
 
 
-def calls_of(core, writes):
-    calls = []
-    for n in sorted({w[3] for w in writes}):
-        off = [w for w in writes if w[3] == n and w[0] // 8 != core // 8]
-        on = [w for w in writes if w[3] == n and w[0] // 8 == core // 8]
-        while off or on:
-            take_off, off = off[:8], off[8:]
-            e_off = 8
-            while take_off and e_off * len(take_off) > 8:
-                e_off //= 2
-            first_on = e_off * len(take_off)
-            take_on, on = on[:16 - first_on], on[16 - first_on:]
-            e_on = 16
-            while take_on and e_on * len(take_on) > 16 - first_on:
-                e_on //= 2
-            call, bit = [], 0
-            for group, e in ((take_off, e_off), (take_on, e_on)):
-                for w in group:
-                    call.append(w + (((1 << e) - 1) << bit, e))
-                    bit += e
-            calls.append(call)
-    return calls
+def engines_of(core, writes):
+    off = [w for w in writes if w[0] // 8 != core // 8]
+    on = [w for w in writes if w[0] // 8 == core // 8]
+    assert len(off) <= 8
+    e_off = 8
+    while off and e_off * len(off) > 8:
+        e_off //= 2
+    first_on = 8 if off else 0
+    e_on = 16
+    while on and e_on * len(on) > 16 - first_on:
+        e_on //= 2
+    out, bit = [], 0
+    for w in off:
+        out.append(w + (((1 << e_off) - 1) << bit, e_off))
+        bit += e_off
+    bit = first_on
+    for w in on:
+        out.append(w + (((1 << e_on) - 1) << bit, e_on))
+        bit += e_on
+    return out
+
+
+ORDER = ("b", "a", "s")
+
+
+def schedule():
+    sched, arriving = {}, {}
+    for core, phases in plan().items():
+        sched[core] = [(cls, engines_of(core, phases[cls])) for cls in ORDER if cls in phases]
+        for cls, call in sched[core]:
+            for t in call:
+                arriving[(t[0], cls)] = arriving.get((t[0], cls), 0) + t[5]
+    return sched, arriving
 
 
 def rank_program(g, core, T, topo):
-    writes = plan()
-    all_calls = {c: calls_of(c, w) for c, w in writes.items()}
-    if core not in all_calls:
+    sched, arriving = schedule()
+    if core not in sched:
         return
-    arriving = sum(t[5] for calls in all_calls.values() for call in calls for t in call if t[0] == core)
     rank = T.rank_of(core)
+    arr = {"a": T.sem.arr_a, "b": T.sem.arr_b, "s": T.sem.arr_s}
+    half = NB * B // 2
 
     if rank is not None:
-        g.dma_start(T.src[:], T.x[:]).then_inc(T.sem.loaded, 16)
+        far = half * (1 - rank // 16)
+        near = half * (rank // 16)
+        g.dma_start(T.src[:, far:far + half], T.x[:, far:far + half]).then_inc(T.sem.ld_far, 16)
+        g.dma_start(T.src[:, near:near + half], T.x[:, near:near + half]).then_inc(T.sem.ld_near, 16)
         g.dma_start(T.land[:, rank * B:(rank + 1) * B], T.x[:, rank * B:(rank + 1) * B]).then_inc(T.sem.own, 16)
-        g.wait_ge(T.sem.loaded, 16)
         source = T.src
     else:
-        g.wait_ge(T.sem.arrived, arriving)
         source = T.land
 
     leaving = 0
-    for call in all_calls[core]:
+    waited = set()
+    for cls, call in sched[core]:
+        if rank is not None:
+            sem = T.sem.ld_near if cls == "s" else T.sem.ld_far
+            if sem not in waited:
+                g.wait_ge(sem, 16)
+                waited.add(sem)
+        else:
+            g.wait_ge(arr[cls], arriving[(core, cls)])
         transfers = []
         for dst, src_col, dst_col, n, mask, engines in call:
             rid, pid = topo.addr(dst, core)
             transfers.append(RemoteDMATransfer(
-                dst_ids=[DstId(rid=rid, pnc=pid)], dma_engine_mask=mask, remote_sem=T.sem.arrived,
+                dst_ids=[DstId(rid=rid, pnc=pid)], dma_engine_mask=mask, remote_sem=arr[cls],
                 src=source[:, src_col:src_col + n * B], dst=T.land[:, dst_col:dst_col + n * B]))
             leaving += engines
         g.remote_dma_fused(transfers, local_sem=T.sem.sent)
 
     if rank is not None:
-        g.wait_ge(T.sem.arrived, arriving)
+        g.wait_ge(T.sem.arr_s, arriving[(core, "s")])
         g.wait_ge(T.sem.own, 16)
-        g.dma_start(T.y[:], T.land[:]).then_inc(T.sem.stored, 16)
-        g.wait_ge(T.sem.stored, 16)
+        g.dma_start(T.y[:, near:near + half], T.land[:, near:near + half]).then_inc(T.sem.stored, 16)
+        g.wait_ge(T.sem.arr_a, arriving[(core, "a")])
+        g.wait_ge(T.sem.arr_b, arriving[(core, "b")])
+        g.dma_start(T.y[:, far:far + half], T.land[:, far:far + half]).then_inc(T.sem.stored, 16)
+        g.wait_ge(T.sem.stored, 32)
     g.wait_ge(T.sem.sent, leaving)

@@ -111,10 +111,10 @@ def rank_program(g, core, T, topo):
     waited = set()
     for cls, call in sched[core]:
         if rank is not None:
-            sem = T.sem.ld_near if cls == "s" else T.sem.ld_far
-            if sem not in waited:
-                g.wait_ge(sem, 16)
-                waited.add(sem)
+            key = "near" if cls == "s" else "far"
+            if key not in waited:
+                g.wait_ge(T.sem.ld_near if cls == "s" else T.sem.ld_far, 16)
+                waited.add(key)
         else:
             g.wait_ge(arr[cls], arriving[(core, cls)])
         transfers = []

from concourse.bass import DstId, RemoteDMATransfer

NB = 32
B = 32

SCRATCH = {
    "src": ("sbuf", [128, NB * B], "float32"),
    "land": ("sbuf", [128, NB * B], "float32"),
}
SEMAPHORES = ["ld_far", "ld_near", "own", "sent", "arr_a", "arr_b", "arr_s", "stored"]

MATE_PORT = (2, 3, 6, 7)


def world(host, chip, core):
    return host * 128 + chip * 8 + core


def rank_core(r):
    h, k, c = r // 16, (r % 16) // 2, r % 2
    return world(h, 2 * k + h, c)


def plan():
    phases = {}
    used = {}

    def put(core, cls, dst, src_col, dst_col, n):
        phases.setdefault(core, {}).setdefault(cls, []).append((dst, src_col, dst_col, n))

    def via(r, cls, helper, first, n):
        slot = used.get(helper, 0)
        used[helper] = slot + n * B
        put(rank_core(r), cls, helper, first * B, slot, n)
        for i in range(n):
            if first + i != r:
                put(helper, cls, rank_core(first + i), slot + i * B, r * B, 1)

    for r in range(NB):
        h, k, c = r // 16, (r % 16) // 2, r % 2
        chip = 2 * k + h
        mine, other = 16 * h, 16 * (1 - h)
        die_a, die_b, die_b_port = world(h, chip, 2 + c), world(h, chip, 4 + c), world(h, chip, 6 + c)
        pair, half = k // 2, k // 4
        for m in range(4 * (1 - half), 4 * (1 - half) + 4):
            via(r, "b", world(1 - h, 2 * m + h, MATE_PORT[k % 4]), other + 2 * m, 2)
        base = other + 8 * half
        via(r, "a", die_a, base + 4 * c, 4)
        via(r, "a", die_b_port, base + 4 * (1 - c), 4)
        via(r, "s", die_a if c == 0 else die_b_port, mine + 4 * pair, 4)
        via(r, "s", die_a, mine + 4 * ((pair + 1) % 4), 4)
        via(r, "s", die_b, mine + 4 * ((pair + 2) % 4), 4)
        via(r, "s", die_b, mine + 4 * ((pair + 3) % 4), 4)
    return phases


def engines_of(core, writes):
    off = [w for w in writes if w[0] // 8 != core // 8]
    on = [w for w in writes if w[0] // 8 == core // 8]
    assert len(off) <= 8
    e_off = 8
    while off and e_off * len(off) > 8:
        e_off //= 2
    first_on = 8 if off else 0
    e_on = 16
    while on and e_on * len(on) > 16 - first_on:
        e_on //= 2
    out, bit = [], 0
    for w in off:
        out.append(w + (((1 << e_off) - 1) << bit, e_off))
        bit += e_off
    bit = first_on
    for w in on:
        out.append(w + (((1 << e_on) - 1) << bit, e_on))
        bit += e_on
    return out


ORDER = ("b", "a", "s")


def schedule():
    sched, arriving = {}, {}
    for core, phases in plan().items():
        sched[core] = [(cls, engines_of(core, phases[cls])) for cls in ORDER if cls in phases]
        for cls, call in sched[core]:
            for t in call:
                arriving[(t[0], cls)] = arriving.get((t[0], cls), 0) + t[5]
    return sched, arriving


def rank_program(g, core, T, topo):
    sched, arriving = schedule()
    if core not in sched:
        return
    rank = T.rank_of(core)
    arr = {"a": T.sem.arr_a, "b": T.sem.arr_b, "s": T.sem.arr_s}
    half = NB * B // 2

    if rank is not None:
        far = half * (1 - rank // 16)
        near = half * (rank // 16)
        g.dma_start(T.src[:, far:far + half], T.x[:, far:far + half]).then_inc(T.sem.ld_far, 16)
        g.dma_start(T.src[:, near:near + half], T.x[:, near:near + half]).then_inc(T.sem.ld_near, 16)
        g.dma_start(T.land[:, rank * B:(rank + 1) * B], T.x[:, rank * B:(rank + 1) * B]).then_inc(T.sem.own, 16)
        source = T.src
    else:
        source = T.land

    leaving = 0
    waited = set()
    for cls, call in sched[core]:
        if rank is not None:
            key = "near" if cls == "s" else "far"
            if key not in waited:
                g.wait_ge(T.sem.ld_near if cls == "s" else T.sem.ld_far, 16)
                waited.add(key)
        else:
            g.wait_ge(arr[cls], arriving[(core, cls)])
        transfers = []
        for dst, src_col, dst_col, n, mask, engines in call:
            rid, pid = topo.addr(dst, core)
            transfers.append(RemoteDMATransfer(
                dst_ids=[DstId(rid=rid, pnc=pid)], dma_engine_mask=mask, remote_sem=arr[cls],
                src=source[:, src_col:src_col + n * B], dst=T.land[:, dst_col:dst_col + n * B]))
            leaving += engines
        g.remote_dma_fused(transfers, local_sem=T.sem.sent)

    if rank is not None:
        g.wait_ge(T.sem.arr_s, arriving[(core, "s")])
        g.wait_ge(T.sem.own, 16)
        g.dma_start(T.y[:, near:near + half], T.land[:, near:near + half]).then_inc(T.sem.stored, 16)
        g.wait_ge(T.sem.arr_a, arriving[(core, "a")])
        g.wait_ge(T.sem.arr_b, arriving[(core, "b")])
        g.dma_start(T.y[:, far:far + half], T.land[:, far:far + half]).then_inc(T.sem.stored, 16)
        g.wait_ge(T.sem.stored, 32)
    g.wait_ge(T.sem.sent, leaving)
